import numpy as np
import ml_dtypes


def mxq(x, axis, fmt="e4m3"):
    dtype, down = {"e4m3": (ml_dtypes.float8_e4m3fn, 7), "e5m2": (ml_dtypes.float8_e5m2, 14)}[fmt]
    v = np.moveaxis(np.asarray(x, np.float32).astype(ml_dtypes.bfloat16).astype(np.float64), axis, -1)
    blocks = v.reshape(v.shape[:-1] + (-1, 32))
    amax = np.abs(blocks).max(-1, keepdims=True)
    byte = np.maximum(np.where(amax > 0, np.frexp(amax)[1] - 1 + 127, 0) - down, 1)
    scale = np.exp2(byte - 127.0)
    codes = (blocks / scale).astype(np.float32).astype(dtype).astype(np.float64)
    return np.moveaxis((codes * scale).reshape(v.shape), -1, axis)


WIDE = False


def mx_kscale(k):
    if not WIDE:
        return np.ones(k)
    levels = np.array([10, -10, 5, -5, 0])
    if k % 512:
        return np.exp2(np.random.permutation(np.resize(levels, k // 32))).repeat(32)
    a = np.empty((k // 512, 16))
    for p in range(k // 512):
        a[p, :8] = np.random.permutation(np.resize(levels, 8))
        for g in range(8):
            far = levels[np.abs(levels - a[p, g]) >= 10]
            a[p, g + 8] = far[np.random.randint(len(far))]
    return np.exp2(a.ravel()).repeat(32)


def f64(x):
    return np.asarray(x).astype(np.float64)


def striped(idx):
    return np.tile(np.asarray(idx).reshape(-1, 16).T, (8, 1)).astype(np.uint16)


def unstriped(offs):
    return offs[:16].T.reshape(-1).astype(np.int64)


E2M1 = np.array([0.0, 0.5, 1.0, 1.5, 2.0, 3.0, 4.0, 6.0, -0.0, -0.5, -1.0, -1.5, -2.0, -3.0, -4.0, -6.0])


def pack_weight(w, fmt):
    k, n = w.shape
    w = f64(np.asarray(w, np.float32).astype(ml_dtypes.bfloat16)).reshape(k // 32, 32, n)
    amax = np.abs(w).max(1)
    if fmt == "e4m3":
        byte = np.frexp(amax)[1] - 1 + 127 - 7
    else:
        mant, ex = np.frexp(amax / 6.0)
        byte = np.where(mant > 0.5, ex, ex - 1) + 127
    byte = np.clip(np.where(amax > 0, byte, 1), 1, 254)
    scaled = (w * np.exp2(127.0 - byte)[:, None, :]).reshape(k, n).astype(np.float32)
    by_word = np.ascontiguousarray(scaled.reshape(k // 512, 128, 4, n).transpose(0, 1, 3, 2))
    if fmt == "e4m3":
        words = by_word.astype(ml_dtypes.float8_e4m3fn).view(np.uint8)
    else:
        c = by_word.astype(ml_dtypes.float4_e2m1fn).view(np.uint8) & 0xF
        words = (c[..., 0::2] | (c[..., 1::2] << 4)).reshape(k // 512, 128, 2 * n)
    return np.ascontiguousarray(words), np.ascontiguousarray(byte.astype(np.uint8).reshape(k // 512, 16, n))


def unpack_weight(words, scales, fmt):
    g, _, n = scales.shape
    words = np.ascontiguousarray(words).reshape(g, 128, n, -1)
    if fmt == "e4m3":
        vals = words.view(ml_dtypes.float8_e4m3fn).astype(np.float64)
    else:
        nib = np.empty((g, 128, n, 4), np.uint8)
        nib[..., 0::2] = words & 0xF
        nib[..., 1::2] = words >> 4
        vals = E2M1[nib]
    vals = vals * np.repeat(np.exp2(scales.astype(np.float64) - 127.0), 8, axis=1)[..., None]
    return vals.transpose(0, 1, 3, 2).reshape(g * 512, n)


def sigmoid(v):
    return 1.0 / (1.0 + np.exp(-v))


D, E, T, I, Q, G = 512, 512, 2048, 512, 128, 64


def setup_inputs():
    n = np.random.standard_normal
    idx = np.random.permutation(T)[:I]
    fd = mx_kscale(D)
    fe = mx_kscale(E)
    fi = mx_kscale(I)
    ti = np.ones(T)
    ti[idx] = fi
    keysp = pack_weight(n((D, T)) / fd[:, None], "e2m1")
    valsp = pack_weight(n((E, T)) / fe[:, None], "e2m1")
    return {
        "query": (n((D, Q)) * 0.6 / np.sqrt(D) * fd[:, None]).astype(np.float32),
        "keys_words": keysp[0],
        "keys_scales": keysp[1],
        "gout": (n((E, Q)) * 1 / np.sqrt(E) * fe[:, None]).astype(np.float32),
        "vals_words": valsp[0],
        "vals_scales": valsp[1],
        "size": (np.random.uniform(0.1, 0.4, (1, I))).astype(np.float32),
        "fs": (np.random.uniform(128.0, 512.0, (1, I)) * fi).astype(np.float32),
        "keyrows": (n((D, T)) / ti).astype(np.float32),
        "res": (n((Q, D)) * 4.0).astype(np.float32),
        "offs": striped(idx),
    }


def reference(query, keys_words, keys_scales, gout, vals_words, vals_scales, size, fs, keyrows, res, offs):
    idx = unstriped(offs)
    keysu = unpack_weight(keys_words, keys_scales, "e2m1")
    valsu = unpack_weight(vals_words, vals_scales, "e2m1")
    queryq = mxq(f64(query), 0, "e4m3")
    keysidxg = keysu[:, idx]
    a = queryq.T @ keysidxg
    s = a.reshape(Q, G, I // G).mean(axis=2)
    p = np.exp(s - np.max(s, axis=1, keepdims=True))
    z = np.sum(p, axis=1, keepdims=True)
    r = p / z
    rr = np.repeat(r, I // G, axis=1)
    goutq = mxq(f64(gout), 0, "e4m3")
    valsidxg = valsu[:, idx]
    c0 = goutq.T @ valsidxg
    drr = c0 * f64(size) * sigmoid(a)
    dr = drr.reshape(Q, G, I // G).sum(axis=2)
    dz = np.sum(dr * p / np.square(z) * (-1.0), axis=1, keepdims=True)
    dp = dr / z + dz
    ds = dp * p
    e1 = ds / 8.0
    r1 = np.repeat(e1, I // G, axis=1)
    da = c0 * f64(size) * rr * sigmoid(a) * (1.0 - sigmoid(a)) + r1
    gs = da * f64(fs)
    gt1 = gs.T
    kt = f64(keyrows)[:, idx].T
    gt1q = mxq(gt1, 0, "e4m3")
    ktq = mxq(kt, 0, "e4m3")
    gq = gt1q.T @ ktq
    y = gq + f64(res)
    return y

@@ -1,0 +1,233 @@
+from contextlib import ExitStack
+
+import concourse.mybir as mybir
+
+D, T, I, Q, G = 512, 2048, 512, 128, 64
+P = 128
+PACK = 4
+SPAN = I // G
+FLOPS = 3 * 2 * 512 * 128 * 512
+
+F32 = mybir.dt.float32
+BF16 = mybir.dt.bfloat16
+I32 = mybir.dt.int32
+U32 = mybir.dt.uint32
+U16 = mybir.dt.uint16
+U8 = mybir.dt.uint8
+FP8X4 = mybir.dt.float8_e4m3fn_x4
+FP4X4 = mybir.dt.float4_e2m1fn_x4
+ALU = mybir.AluOpType
+ACT = mybir.ActivationFunctionType
+AX = mybir.AxisListType
+
+
+def tile_attend_bspanread_q_kernel(tc, query, keys_words, keys_scales, gout, vals_words, vals_scales, size, fs, keyrows, res, offs, out):
+    nc = tc.nc
+    with ExitStack() as ctx:
+        sb = ctx.enter_context(tc.tile_pool(name="sb", bufs=1))
+        late = ctx.enter_context(tc.tile_pool(name="late", bufs=1))
+        ps = ctx.enter_context(tc.psum_pool(name="ps", bufs=1))
+
+        def tile(name, shape, dtype, after=None):
+            return sb.tile(shape, dtype, name=name, tag=after or name, align_bytes=64)
+
+        offsets = sb.tile([P, I // 16], U16, name="offsets")
+        ks_pool = tile("ks_pool", [P, T], U8)
+        vs_pool = late.tile([P, T], U8, name="vs_pool", align_bytes=64, offset=0)
+        kw_pool = tile("kw_pool", [P, T], U16)
+        vw_pool = tile("vw_pool", [P, T], U16)
+        q_raw = tile("q_raw", [P, PACK * Q], F32)
+        g_raw = tile("g_raw", [P, PACK * Q], F32)
+        rows = [tile("rows%d" % b, [P, T], F32) for b in range(3)]
+        rows.append(late.tile([P, T], F32, name="rows3", align_bytes=64, offset=4096))
+        res_sb = tile("res_sb", [P, D], F32)
+        size_col = tile("size_col", [P, PACK], F32)
+        fs_col = tile("fs_col", [P, PACK], F32)
+        ident = tile("ident", [P, P], F32)
+        warm_in = tile("warm_in", [P, 1], F32)
+        warm_out = tile("warm_out", [P, 1], F32)
+
+        def load_scales(queues, pool_tile, scales):
+            for quad in range(4):
+                queues[quad].dma_start(
+                    out=pool_tile[32 * quad : 32 * quad + 4, :].bitcast(I32),
+                    in_=scales[0, 4 * quad : 4 * quad + 4, :].bitcast(I32),
+                )
+
+        nc.vector.memset(ks_pool[:].bitcast(I32), 0)
+        nc.vector.memset(warm_in[:], 0.0)
+        nc.vector.memset(vs_pool[:].bitcast(I32), 0)
+        nc.sync.dma_start(offsets[:], offs)
+        nc.sync.dma_start(out=kw_pool[:].bitcast(I32), in_=keys_words[0].bitcast(I32))
+        load_scales([nc.sync] * 4, ks_pool, keys_scales)
+        nc.sync.dma_start(out=q_raw[:], in_=query.rearrange("(p j) w -> p (j w)", j=PACK))
+        nc.sync.dma_start(out=g_raw[:], in_=gout.rearrange("(p j) w -> p (j w)", j=PACK))
+        nc.sync.dma_start(out=vw_pool[:].bitcast(I32), in_=vals_words[0].bitcast(I32))
+        nc.scalar.activation(warm_out[:], warm_in[:], ACT.Exp)
+        nc.sync.dma_start(out=size_col[:], in_=size.rearrange("o (p t) -> (o p) t", t=PACK))
+        load_scales([nc.sync] * 4, vs_pool, vals_scales)
+        for b in range(4):
+            nc.sync.dma_start(out=rows[b][:], in_=keyrows[b * P : (b + 1) * P, :])
+            if b == 1:
+                nc.sync.dma_start(out=fs_col[:], in_=fs.rearrange("o (p t) -> (o p) t", t=PACK))
+        nc.sync.dma_start(out=res_sb[:], in_=res)
+        ones = tile("ones", [P, 32], F32)
+        count = tile("count", [P, 32], F32)
+        count_t = tile("count_t", [P, 32], F32)
+        nc.vector.memset(ones[:], 1.0)
+        nc.vector.memset(ident[:], 0.0)
+        nc.vector.tensor_tensor_scan(count[:], ones[:], ones[:], 0.0, ALU.mult, ALU.add)
+        nc.vector.transpose(count_t[:], count[:])
+        for quad in range(4):
+            part = slice(32 * quad, 32 * quad + 32)
+            nc.vector.tensor_tensor(ident[part, part], count[part, :], count_t[part, :], ALU.is_equal)
+
+        def quantize(name, grouped):
+            codes = tile(name + "_codes", [P, P], U32)
+            scales = tile(name + "_scales", [P, P], U8)
+            nc.vector.quantize_mx(out=codes[:].bitcast(FP8X4), scales=scales[:], in_=grouped[:])
+            return codes, scales
+
+        def group_rows(grouped, raw):
+            nc.scalar.copy(
+                out=grouped.rearrange("p (w j) -> p w j", j=PACK),
+                in_=raw[:].rearrange("p (j w) -> p w j", j=PACK),
+            )
+
+        def gather(name, pool_tile, dtype):
+            picked = tile(name, [P, I], dtype)
+            nc.vector.tensor_copy(picked[:], pool_tile[:].indirect(offsets[:]))
+            return picked
+
+        def scores(name, stat, words, scales):
+            acc = ps.tile([P, I], F32, name=name)
+            nc.tensor.matmul_mx(
+                out=acc[:], lhsT=qg_codes[:, stat].bitcast(FP8X4), lhsT_scale=qg_scales[:, stat],
+                rhs=words[:].bitcast(FP4X4), rhs_scale=scales[:], start=True, stop=True,
+            )
+            return acc
+
+        def dealt(acc):
+            return acc[:].rearrange("q (p t) -> q t p", t=PACK)
+
+        def by_place(x):
+            return x[:].rearrange("q (t p) -> q t p", t=PACK)
+
+        kw = gather("kw", kw_pool, U16)
+        ks = gather("ks", ks_pool, U8)
+        qg = tile("qg_grouped", [P, 2 * PACK * Q], BF16)
+        group_rows(qg[:, 0 : PACK * Q], q_raw)
+        group_rows(qg[:, PACK * Q : 2 * PACK * Q], g_raw)
+        qg_codes = tile("qg_codes", [P, 2 * Q], U32)
+        qg_scales = tile("qg_scales", [P, 2 * Q], U8)
+        nc.vector.quantize_mx(out=qg_codes[:].bitcast(FP8X4), scales=qg_scales[:], in_=qg[:])
+        a = scores("a", slice(0, Q), kw, ks)
+        size_ps = ps.tile([P, I], F32, name="size_ps")
+        for t in range(PACK):
+            nc.tensor.transpose(size_ps[:, t * P : (t + 1) * P], size_col[:, t : t + 1].to_broadcast([P, P]), ident[:])
+
+        vw = gather("vw", vw_pool, U16)
+        vs = gather("vs", vs_pool, U8)
+        c0 = scores("c0", slice(Q, 2 * Q), vw, vs)
+
+        th = tile("th", [P, I], F32)
+        nc.scalar.activation(by_place(th), dealt(a), ACT.Tanh, scale=0.5)
+        s_sum = tile("s_sum", [P, G], F32, after="vw_pool")
+        nc.vector.tensor_reduce(s_sum[:], a[:].rearrange("q (g j) -> q g j", j=SPAN), AX.X, ALU.add)
+        s_neg = tile("s_neg", [P, G], F32)
+        m_neg = tile("m_neg", [P, 1], F32)
+        nc.vector.tensor_scalar(s_neg[:], s_sum[:], -1.0 / SPAN, None, ALU.mult, ALU.min, accum_out=m_neg[:])
+        p_exp = tile("p_exp", [P, G], F32)
+        z = tile("z", [P, 1], F32)
+        nc.scalar.activation(p_exp[:], s_neg[:], ACT.Exp, bias=m_neg[:], scale=-1.0, accum_out=z[:])
+
+
+        u = late.tile([P, I], F32, name="u", align_bytes=64, offset=64)
+        nc.vector.scalar_tensor_tensor(u[:], th[:], 1.0, size_ps[:], ALU.add, ALU.mult)
+        rz = late.tile([P, 1], F32, name="rz", align_bytes=64, offset=0)
+        nc.vector.reciprocal(rz[:], z[:])
+        drr = tile("drr", [P, I], F32)
+        nc.vector.tensor_tensor(by_place(drr), dealt(c0), by_place(u), ALU.mult)
+        r2 = tile("r2", [P, P], F32)
+        nc.scalar.activation(
+            r2[:].rearrange("q (g h) -> q g h", h=2), p_exp[:].unsqueeze(2).to_broadcast([P, G, 2]),
+            ACT.Copy, scale=rz[:],
+        )
+        dr = tile("dr", [P, G], F32)
+        nc.vector.tensor_reduce(dr[:], drr[:].rearrange("q (t g h) -> q g t h", t=PACK, h=2), AX.XY, ALU.add)
+        v = tile("v", [P, I], F32)
+        nc.vector.scalar_tensor_tensor(
+            by_place(v), by_place(th), -1.0, r2[:].unsqueeze(1).to_broadcast([P, PACK, P]), ALU.add, ALU.mult
+        )
+        e = tile("e", [P, G], F32)
+        e_sum = tile("e_sum", [P, 1], F32)
+        nc.vector.scalar_tensor_tensor(e[:], dr[:], 0.25, r2[:, 0:P:2], ALU.mult, ALU.mult, accum_out=e_sum[:])
+        y = tile("y", [P, I], F32)
+        nc.vector.tensor_tensor(y[:], v[:], drr[:], ALU.mult)
+        f2 = tile("f2", [P, P], F32)
+        nc.vector.scalar_tensor_tensor(
+            f2[:].rearrange("q (g h) -> q g h", h=2), r2[:].rearrange("q (g h) -> q g h", h=2), e_sum[:],
+            e[:].unsqueeze(2).to_broadcast([P, G, 2]), ALU.mult, ALU.subtract,
+        )
+        da_t = ps.tile([P, I], F32, name="da_t")
+        for t in range(PACK):
+            nc.tensor.matmul(da_t[:, t * P : (t + 1) * P], y[:, t * P : (t + 1) * P], ident[:],
+                             start=(t == 0), stop=False, is_transpose=True)
+        for t in range(PACK):
+            nc.tensor.matmul(da_t[:, t * P : (t + 1) * P], f2[:], ident[:],
+                             start=False, stop=(t == PACK - 1), is_transpose=True)
+
+        def gather_rows(b, grouped):
+            if b == 0:
+                rows_bf = tile("rows_bf", [P, T], BF16)
+                nc.scalar.copy(out=rows_bf[:], in_=rows[b][:])
+                picked = tile("picked%d" % b, [P, I], BF16)
+                nc.scalar.activation(picked[:], rows_bf[:].indirect(offsets[:]), ACT.Copy)
+            else:
+                picked = gather("picked%d" % b, rows[b], BF16)
+            turned = ps.tile([P, 2 * P], F32, name="turned", tag="turned", bufs=2)
+            words = picked[:].bitcast(F32)
+            for h in range(2):
+                nc.tensor.transpose(turned[:, h * P : (h + 1) * P], words[:, h : 2 * P : 2], ident[:])
+            nc.scalar.copy(
+                out=grouped.bitcast(F32).rearrange("p (d h) -> p d h", h=2),
+                in_=turned[:].rearrange("p (h d) -> p d h", h=2),
+            )
+
+        kt01 = tile("kt01_grouped", [P, 2 * I], BF16)
+        gt_kt2 = late.tile([P, 2 * I], BF16, name="gt_kt2_grouped", align_bytes=64, offset=4096)
+        kt3 = tile("kt3_grouped", [P, I], BF16)
+        gather_rows(0, kt01[:, 0:I])
+        gather_rows(1, kt01[:, I : 2 * I])
+        gather_rows(2, gt_kt2[:, I : 2 * I])
+        gather_rows(3, kt3[:])
+        nc.vector.scalar_tensor_tensor(
+            gt_kt2[:, 0:I].rearrange("p (q t) -> p q t", t=PACK), da_t[:].rearrange("p (t q) -> p q t", t=PACK), -0.25,
+            fs_col[:].unsqueeze(1).to_broadcast([P, Q, PACK]), ALU.mult, ALU.mult,
+        )
+        kt01_codes = late.tile([P, 2 * P], U32, name="kt01_codes", align_bytes=64, offset=4096 + 2048)
+        kt01_scales = tile("kt01_scales", [P, 2 * P], U8)
+        nc.vector.quantize_mx(out=kt01_codes[:].bitcast(FP8X4), scales=kt01_scales[:], in_=kt01[:])
+        gk_codes = tile("gk_codes", [P, 2 * P], U32)
+        gk_scales = tile("gk_scales", [P, 2 * P], U8)
+        nc.vector.quantize_mx(out=gk_codes[:].bitcast(FP8X4), scales=gk_scales[:], in_=gt_kt2[:])
+        kt3_codes, kt3_scales = quantize("kt3", kt3)
+
+        def product(acc, codes, scales):
+            nc.tensor.matmul_mx(
+                out=acc, lhsT=gk_codes[:, 0:P].bitcast(FP8X4), lhsT_scale=gk_scales[:, 0:P],
+                rhs=codes.bitcast(FP8X4), rhs_scale=scales, start=True, stop=True,
+            )
+
+        def finish(name, acc, cols):
+            result = tile(name, [P, 2 * P], F32)
+            nc.vector.tensor_tensor(result[:], acc[:], res_sb[:, cols], ALU.add)
+            nc.sync.dma_start(out=out[:, cols], in_=result[:])
+
+        gq_low = ps.tile([P, 2 * P], F32, name="gq_low")
+        product(gq_low[:], kt01_codes[:], kt01_scales[:])
+        gq_high = ps.tile([P, 2 * P], F32, name="gq_high")
+        product(gq_high[:, 0:P], gk_codes[:, P : 2 * P], gk_scales[:, P : 2 * P])
+        product(gq_high[:, P : 2 * P], kt3_codes[:], kt3_scales[:])
+        finish("result_low", gq_low, slice(0, 2 * P))
+        finish("result_high", gq_high, slice(2 * P, 4 * P))

@@ -38,8 +38,11 @@ def tile_attend_bspanread_q_kernel(tc, query, keys_words, keys_scales, gout, val
         vw_pool = tile("vw_pool", [P, T], U16)
         q_raw = tile("q_raw", [P, PACK * Q], F32)
         g_raw = tile("g_raw", [P, PACK * Q], F32)
-        rows = [tile("rows%d" % b, [P, T], F32) for b in range(3)]
-        rows.append(late.tile([P, T], F32, name="rows3", align_bytes=64, offset=4096))
+        half = T // 2
+        rows0_low = late.tile([P, half], F32, name="rows0_low", align_bytes=64, offset=4096)
+        rows0_high = tile("rows0_high", [P, half], F32)
+        rows = [None, tile("rows1", [P, T], F32), tile("rows2", [P, T], F32)]
+        rows.append(late.tile([P, T], F32, name="rows3", align_bytes=64, offset=8192))
         res_sb = tile("res_sb", [P, D], F32)
         size_col = tile("size_col", [P, PACK], F32)
         fs_col = tile("fs_col", [P, PACK], F32)
@@ -60,16 +63,17 @@ def tile_attend_bspanread_q_kernel(tc, query, keys_words, keys_scales, gout, val
         nc.sync.dma_start(offsets[:], offs)
         nc.sync.dma_start(out=kw_pool[:].bitcast(I32), in_=keys_words[0].bitcast(I32))
         load_scales([nc.sync] * 4, ks_pool, keys_scales)
+        nc.sync.dma_start(out=vw_pool[:].bitcast(I32), in_=vals_words[0].bitcast(I32))
         nc.sync.dma_start(out=q_raw[:], in_=query.rearrange("(p j) w -> p (j w)", j=PACK))
         nc.sync.dma_start(out=g_raw[:], in_=gout.rearrange("(p j) w -> p (j w)", j=PACK))
-        nc.sync.dma_start(out=vw_pool[:].bitcast(I32), in_=vals_words[0].bitcast(I32))
         nc.scalar.activation(warm_out[:], warm_in[:], ACT.Exp)
-        nc.sync.dma_start(out=size_col[:], in_=size.rearrange("o (p t) -> (o p) t", t=PACK))
         load_scales([nc.sync] * 4, vs_pool, vals_scales)
-        for b in range(4):
+        nc.gpsimd.dma_start(out=size_col[:], in_=size.rearrange("o (p t) -> (o p) t", t=PACK))
+        nc.sync.dma_start(out=rows0_low[:], in_=keyrows[0:P, 0:half])
+        nc.sync.dma_start(out=rows0_high[:], in_=keyrows[0:P, half:T])
+        nc.gpsimd.dma_start(out=fs_col[:], in_=fs.rearrange("o (p t) -> (o p) t", t=PACK))
+        for b in range(1, 4):
             nc.sync.dma_start(out=rows[b][:], in_=keyrows[b * P : (b + 1) * P, :])
-            if b == 1:
-                nc.sync.dma_start(out=fs_col[:], in_=fs.rearrange("o (p t) -> (o p) t", t=PACK))
         nc.sync.dma_start(out=res_sb[:], in_=res)
         ones = tile("ones", [P, 32], F32)
         count = tile("count", [P, 32], F32)
@@ -82,27 +86,28 @@ def tile_attend_bspanread_q_kernel(tc, query, keys_words, keys_scales, gout, val
             part = slice(32 * quad, 32 * quad + 32)
             nc.vector.tensor_tensor(ident[part, part], count[part, :], count_t[part, :], ALU.is_equal)
 
-        def quantize(name, grouped):
-            codes = tile(name + "_codes", [P, P], U32)
-            scales = tile(name + "_scales", [P, P], U8)
+        def quantize(name, grouped, codes):
+            scales = tile(name, [P, codes.shape[1]], U8)
             nc.vector.quantize_mx(out=codes[:].bitcast(FP8X4), scales=scales[:], in_=grouped[:])
-            return codes, scales
+            return scales
 
-        def group_rows(grouped, raw):
+        def group_rows(name, raw):
+            grouped = tile(name, [P, PACK * Q], BF16)
             nc.scalar.copy(
-                out=grouped.rearrange("p (w j) -> p w j", j=PACK),
+                out=grouped[:].rearrange("p (w j) -> p w j", j=PACK),
                 in_=raw[:].rearrange("p (j w) -> p w j", j=PACK),
             )
+            return grouped
 
         def gather(name, pool_tile, dtype):
             picked = tile(name, [P, I], dtype)
             nc.vector.tensor_copy(picked[:], pool_tile[:].indirect(offsets[:]))
             return picked
 
-        def scores(name, stat, words, scales):
+        def scores(name, codes, code_scales, words, scales):
             acc = ps.tile([P, I], F32, name=name)
             nc.tensor.matmul_mx(
-                out=acc[:], lhsT=qg_codes[:, stat].bitcast(FP8X4), lhsT_scale=qg_scales[:, stat],
+                out=acc[:], lhsT=codes[:].bitcast(FP8X4), lhsT_scale=code_scales[:],
                 rhs=words[:].bitcast(FP4X4), rhs_scale=scales[:], start=True, stop=True,
             )
             return acc
@@ -115,60 +120,60 @@ def tile_attend_bspanread_q_kernel(tc, query, keys_words, keys_scales, gout, val
 
         kw = gather("kw", kw_pool, U16)
         ks = gather("ks", ks_pool, U8)
-        qg = tile("qg_grouped", [P, 2 * PACK * Q], BF16)
-        group_rows(qg[:, 0 : PACK * Q], q_raw)
-        group_rows(qg[:, PACK * Q : 2 * PACK * Q], g_raw)
-        qg_codes = tile("qg_codes", [P, 2 * Q], U32)
-        qg_scales = tile("qg_scales", [P, 2 * Q], U8)
-        nc.vector.quantize_mx(out=qg_codes[:].bitcast(FP8X4), scales=qg_scales[:], in_=qg[:])
-        a = scores("a", slice(0, Q), kw, ks)
-        size_ps = ps.tile([P, I], F32, name="size_ps")
+        vw = gather("vw", vw_pool, U16)
+        q_codes = tile("q_codes", [P, Q], U32)
+        q_scales = quantize("q_scales", group_rows("q_grouped", q_raw), q_codes)
+        a = scores("a", q_codes, q_scales, kw, ks)
+        size_ps = ps.tile([P, I], F32, name="size_ps", tag="small")
         for t in range(PACK):
             nc.tensor.transpose(size_ps[:, t * P : (t + 1) * P], size_col[:, t : t + 1].to_broadcast([P, P]), ident[:])
-
-        vw = gather("vw", vw_pool, U16)
         vs = gather("vs", vs_pool, U8)
-        c0 = scores("c0", slice(Q, 2 * Q), vw, vs)
+        g_codes = late.tile([P, Q], U32, name="g_codes", align_bytes=64, offset=0)
+        g_scales = quantize("g_scales", group_rows("g_grouped", g_raw), g_codes)
+        c0 = scores("c0", g_codes, g_scales, vw, vs)
 
         th = tile("th", [P, I], F32)
         nc.scalar.activation(by_place(th), dealt(a), ACT.Tanh, scale=0.5)
-        s_sum = tile("s_sum", [P, G], F32, after="vw_pool")
+        s_sum = late.tile([P, G], F32, name="s_sum", align_bytes=64, offset=512)
         nc.vector.tensor_reduce(s_sum[:], a[:].rearrange("q (g j) -> q g j", j=SPAN), AX.X, ALU.add)
+        u = late.tile([P, I], F32, name="u", align_bytes=64, offset=1024)
+        nc.vector.scalar_tensor_tensor(u[:], th[:], 1.0, size_ps[:], ALU.add, ALU.mult)
         s_neg = tile("s_neg", [P, G], F32)
         m_neg = tile("m_neg", [P, 1], F32)
         nc.vector.tensor_scalar(s_neg[:], s_sum[:], -1.0 / SPAN, None, ALU.mult, ALU.min, accum_out=m_neg[:])
-        p_exp = tile("p_exp", [P, G], F32)
-        z = tile("z", [P, 1], F32)
-        nc.scalar.activation(p_exp[:], s_neg[:], ACT.Exp, bias=m_neg[:], scale=-1.0, accum_out=z[:])
+        rows_bf = tile("rows_bf", [P, T], BF16)
+        nc.scalar.copy(out=rows_bf[:, 0:half], in_=rows0_low[:])
 
+        def twice(x):
+            return x[:].unsqueeze(2).to_broadcast([P, G, 2])
 
-        u = late.tile([P, I], F32, name="u", align_bytes=64, offset=64)
-        nc.vector.scalar_tensor_tensor(u[:], th[:], 1.0, size_ps[:], ALU.add, ALU.mult)
-        rz = late.tile([P, 1], F32, name="rz", align_bytes=64, offset=0)
-        nc.vector.reciprocal(rz[:], z[:])
+        def pairs(x):
+            return x[:].rearrange("q (g h) -> q g h", h=2)
+
+        p2 = late.tile([P, P], F32, name="p2", align_bytes=64, offset=4096)
+        z2 = tile("z2", [P, 1], F32)
+        nc.scalar.activation(pairs(p2), twice(s_neg), ACT.Exp, bias=m_neg[:], scale=-1.0, accum_out=z2[:])
+        rest = late.tile([P, I], F32, name="rest", align_bytes=64, offset=4096 + 512)
+        nc.scalar.activation(rest[:], th[:], ACT.Identity, bias=4.0, scale=-4.0)
+
         drr = tile("drr", [P, I], F32)
         nc.vector.tensor_tensor(by_place(drr), dealt(c0), by_place(u), ALU.mult)
+        rz = tile("rz", [P, 1], F32)
+        nc.vector.reciprocal(rz[:], z2[:])
         r2 = tile("r2", [P, P], F32)
-        nc.scalar.activation(
-            r2[:].rearrange("q (g h) -> q g h", h=2), p_exp[:].unsqueeze(2).to_broadcast([P, G, 2]),
-            ACT.Copy, scale=rz[:],
-        )
+        nc.scalar.activation(r2[:], p2[:], ACT.Copy, scale=rz[:])
+        p_t = ps.tile([P, P], F32, name="p_t", tag="small")
+        nc.tensor.transpose(p_t[:], r2[:], ident[:])
+        y = tile("y", [P, I], F32)
+        nc.gpsimd.tensor_tensor(y[:], rest[:], drr[:], ALU.mult)
         dr = tile("dr", [P, G], F32)
         nc.vector.tensor_reduce(dr[:], drr[:].rearrange("q (t g h) -> q g t h", t=PACK, h=2), AX.XY, ALU.add)
-        v = tile("v", [P, I], F32)
-        nc.vector.scalar_tensor_tensor(
-            by_place(v), by_place(th), -1.0, r2[:].unsqueeze(1).to_broadcast([P, PACK, P]), ALU.add, ALU.mult
-        )
-        e = tile("e", [P, G], F32)
+        picked1 = gather("picked1", rows[1], BF16)
+        e = tile("e", [P, P], F32, after="rows1")
         e_sum = tile("e_sum", [P, 1], F32)
-        nc.vector.scalar_tensor_tensor(e[:], dr[:], 0.25, r2[:, 0:P:2], ALU.mult, ALU.mult, accum_out=e_sum[:])
-        y = tile("y", [P, I], F32)
-        nc.vector.tensor_tensor(y[:], v[:], drr[:], ALU.mult)
+        nc.vector.scalar_tensor_tensor(pairs(e), twice(dr), rz[:], pairs(p2), ALU.mult, ALU.mult, accum_out=e_sum[:])
         f2 = tile("f2", [P, P], F32)
-        nc.vector.scalar_tensor_tensor(
-            f2[:].rearrange("q (g h) -> q g h", h=2), r2[:].rearrange("q (g h) -> q g h", h=2), e_sum[:],
-            e[:].unsqueeze(2).to_broadcast([P, G, 2]), ALU.mult, ALU.subtract,
-        )
+        nc.vector.tensor_scalar(pairs(f2), twice(dr), e_sum[:], None, ALU.subtract)
         da_t = ps.tile([P, I], F32, name="da_t")
         for t in range(PACK):
             nc.tensor.matmul(da_t[:, t * P : (t + 1) * P], y[:, t * P : (t + 1) * P], ident[:],
@@ -177,15 +182,20 @@ def tile_attend_bspanread_q_kernel(tc, query, keys_words, keys_scales, gout, val
             nc.tensor.matmul(da_t[:, t * P : (t + 1) * P], f2[:], ident[:],
                              start=False, stop=(t == PACK - 1), is_transpose=True)
 
+        nc.scalar.copy(out=rows_bf[:, half:T], in_=rows0_high[:])
+        factor = tile("factor", [P, I], F32, after="rows0_high")
+        for t in range(PACK):
+            nc.scalar.activation(factor[:, t * P : (t + 1) * P], p_t[:], ACT.Copy, scale=fs_col[:, t : t + 1])
+
         def gather_rows(b, grouped):
             if b == 0:
-                rows_bf = tile("rows_bf", [P, T], BF16)
-                nc.scalar.copy(out=rows_bf[:], in_=rows[b][:])
                 picked = tile("picked%d" % b, [P, I], BF16)
                 nc.scalar.activation(picked[:], rows_bf[:].indirect(offsets[:]), ACT.Copy)
+            elif b == 1:
+                picked = picked1
             else:
                 picked = gather("picked%d" % b, rows[b], BF16)
-            turned = ps.tile([P, 2 * P], F32, name="turned", tag="turned", bufs=2)
+            turned = ps.tile([P, 2 * P], F32, name="turned", tag="turned", bufs=4)
             words = picked[:].bitcast(F32)
             for h in range(2):
                 nc.tensor.transpose(turned[:, h * P : (h + 1) * P], words[:, h : 2 * P : 2], ident[:])
@@ -195,23 +205,24 @@ def tile_attend_bspanread_q_kernel(tc, query, keys_words, keys_scales, gout, val
             )
 
         kt01 = tile("kt01_grouped", [P, 2 * I], BF16)
-        gt_kt2 = late.tile([P, 2 * I], BF16, name="gt_kt2_grouped", align_bytes=64, offset=4096)
+        gt_kt2 = late.tile([P, 2 * I], BF16, name="gt_kt2_grouped", align_bytes=64, offset=8192)
         kt3 = tile("kt3_grouped", [P, I], BF16)
         gather_rows(0, kt01[:, 0:I])
         gather_rows(1, kt01[:, I : 2 * I])
         gather_rows(2, gt_kt2[:, I : 2 * I])
         gather_rows(3, kt3[:])
         nc.vector.scalar_tensor_tensor(
-            gt_kt2[:, 0:I].rearrange("p (q t) -> p q t", t=PACK), da_t[:].rearrange("p (t q) -> p q t", t=PACK), -0.25,
-            fs_col[:].unsqueeze(1).to_broadcast([P, Q, PACK]), ALU.mult, ALU.mult,
+            gt_kt2[:, 0:I].rearrange("p (q t) -> p q t", t=PACK), da_t[:].rearrange("p (t q) -> p q t", t=PACK), 0.125,
+            factor[:].rearrange("p (t q) -> p q t", t=PACK), ALU.mult, ALU.mult,
         )
-        kt01_codes = late.tile([P, 2 * P], U32, name="kt01_codes", align_bytes=64, offset=4096 + 2048)
+        kt01_codes = late.tile([P, 2 * P], U32, name="kt01_codes", align_bytes=64, offset=8192 + 2048)
         kt01_scales = tile("kt01_scales", [P, 2 * P], U8)
         nc.vector.quantize_mx(out=kt01_codes[:].bitcast(FP8X4), scales=kt01_scales[:], in_=kt01[:])
         gk_codes = tile("gk_codes", [P, 2 * P], U32)
         gk_scales = tile("gk_scales", [P, 2 * P], U8)
         nc.vector.quantize_mx(out=gk_codes[:].bitcast(FP8X4), scales=gk_scales[:], in_=gt_kt2[:])
-        kt3_codes, kt3_scales = quantize("kt3", kt3)
+        kt3_codes = tile("kt3_codes", [P, P], U32)
+        kt3_scales = quantize("kt3_scales", kt3, kt3_codes)
 
         def product(acc, codes, scales):
             nc.tensor.matmul_mx(
@@ -224,9 +235,9 @@ def tile_attend_bspanread_q_kernel(tc, query, keys_words, keys_scales, gout, val
             nc.vector.tensor_tensor(result[:], acc[:], res_sb[:, cols], ALU.add)
             nc.sync.dma_start(out=out[:, cols], in_=result[:])
 
-        gq_low = ps.tile([P, 2 * P], F32, name="gq_low")
+        gq_low = ps.tile([P, 2 * P], F32, name="gq_low", tag="a")
         product(gq_low[:], kt01_codes[:], kt01_scales[:])
-        gq_high = ps.tile([P, 2 * P], F32, name="gq_high")
+        gq_high = ps.tile([P, 2 * P], F32, name="gq_high", tag="c0")
         product(gq_high[:, 0:P], gk_codes[:, P : 2 * P], gk_scales[:, P : 2 * P])
         product(gq_high[:, P : 2 * P], kt3_codes[:], kt3_scales[:])
         finish("result_low", gq_low, slice(0, 2 * P))

@@ -41,8 +41,7 @@ def tile_attend_bspanread_q_kernel(tc, query, keys_words, keys_scales, gout, val
         half = T // 2
         rows0_low = late.tile([P, half], F32, name="rows0_low", align_bytes=64, offset=4096)
         rows0_high = tile("rows0_high", [P, half], F32)
-        rows = [None, tile("rows1", [P, T], F32), tile("rows2", [P, T], F32)]
-        rows.append(late.tile([P, T], F32, name="rows3", align_bytes=64, offset=8192))
+        rows = [None] + [tile("rows%d" % b, [P, T], F32) for b in range(1, 4)]
         res_sb = tile("res_sb", [P, D], F32)
         size_col = tile("size_col", [P, PACK], F32)
         fs_col = tile("fs_col", [P, PACK], F32)
@@ -51,10 +50,10 @@ def tile_attend_bspanread_q_kernel(tc, query, keys_words, keys_scales, gout, val
         warm_out = tile("warm_out", [P, 1], F32)
 
         def load_scales(queues, pool_tile, scales):
-            for quad in range(4):
-                queues[quad].dma_start(
-                    out=pool_tile[32 * quad : 32 * quad + 4, :].bitcast(I32),
-                    in_=scales[0, 4 * quad : 4 * quad + 4, :].bitcast(I32),
+            for r in range(4):
+                queues[r].dma_start(
+                    out=pool_tile[r:P:32, :].bitcast(I32),
+                    in_=scales[0, r:16:4, :].bitcast(I32),
                 )
 
         nc.vector.memset(ks_pool[:].bitcast(I32), 0)
@@ -67,9 +66,9 @@ def tile_attend_bspanread_q_kernel(tc, query, keys_words, keys_scales, gout, val
         nc.sync.dma_start(out=q_raw[:], in_=query.rearrange("(p j) w -> p (j w)", j=PACK))
         nc.sync.dma_start(out=g_raw[:], in_=gout.rearrange("(p j) w -> p (j w)", j=PACK))
         nc.scalar.activation(warm_out[:], warm_in[:], ACT.Exp)
-        load_scales([nc.sync] * 4, vs_pool, vals_scales)
         nc.gpsimd.dma_start(out=size_col[:], in_=size.rearrange("o (p t) -> (o p) t", t=PACK))
         nc.sync.dma_start(out=rows0_low[:], in_=keyrows[0:P, 0:half])
+        load_scales([nc.sync] * 4, vs_pool, vals_scales)
         nc.sync.dma_start(out=rows0_high[:], in_=keyrows[0:P, half:T])
         nc.gpsimd.dma_start(out=fs_col[:], in_=fs.rearrange("o (p t) -> (o p) t", t=PACK))
         for b in range(1, 4):
@@ -204,41 +203,36 @@ def tile_attend_bspanread_q_kernel(tc, query, keys_words, keys_scales, gout, val
                 in_=turned[:].rearrange("p (h d) -> p d h", h=2),
             )
 
-        kt01 = tile("kt01_grouped", [P, 2 * I], BF16)
-        gt_kt2 = late.tile([P, 2 * I], BF16, name="gt_kt2_grouped", align_bytes=64, offset=8192)
-        kt3 = tile("kt3_grouped", [P, I], BF16)
-        gather_rows(0, kt01[:, 0:I])
-        gather_rows(1, kt01[:, I : 2 * I])
-        gather_rows(2, gt_kt2[:, I : 2 * I])
-        gather_rows(3, kt3[:])
+        first = tile("first_grouped", [P, 4 * I], BF16, after="rows2")
+        last = tile("last_grouped", [P, I], BF16)
+        gather_rows(0, first[:, I : 2 * I])
+        gather_rows(1, first[:, 2 * I : 3 * I])
         nc.vector.scalar_tensor_tensor(
-            gt_kt2[:, 0:I].rearrange("p (q t) -> p q t", t=PACK), da_t[:].rearrange("p (t q) -> p q t", t=PACK), 0.125,
+            first[:, 0:I].rearrange("p (q t) -> p q t", t=PACK), da_t[:].rearrange("p (t q) -> p q t", t=PACK), 0.125,
             factor[:].rearrange("p (t q) -> p q t", t=PACK), ALU.mult, ALU.mult,
         )
-        kt01_codes = late.tile([P, 2 * P], U32, name="kt01_codes", align_bytes=64, offset=8192 + 2048)
-        kt01_scales = tile("kt01_scales", [P, 2 * P], U8)
-        nc.vector.quantize_mx(out=kt01_codes[:].bitcast(FP8X4), scales=kt01_scales[:], in_=kt01[:])
-        gk_codes = tile("gk_codes", [P, 2 * P], U32)
-        gk_scales = tile("gk_scales", [P, 2 * P], U8)
-        nc.vector.quantize_mx(out=gk_codes[:].bitcast(FP8X4), scales=gk_scales[:], in_=gt_kt2[:])
-        kt3_codes = tile("kt3_codes", [P, P], U32)
-        kt3_scales = quantize("kt3_scales", kt3, kt3_codes)
+        gather_rows(2, first[:, 3 * I : 4 * I])
+        gather_rows(3, last[:])
+        first_codes = tile("first_codes", [P, I], U32, after="rows3")
+        first_scales = quantize("first_scales", first, first_codes)
+        last_codes = tile("last_codes", [P, P], U32)
+        last_scales = quantize("last_scales", last, last_codes)
 
         def product(acc, codes, scales):
             nc.tensor.matmul_mx(
-                out=acc, lhsT=gk_codes[:, 0:P].bitcast(FP8X4), lhsT_scale=gk_scales[:, 0:P],
+                out=acc, lhsT=first_codes[:, 0:P].bitcast(FP8X4), lhsT_scale=first_scales[:, 0:P],
                 rhs=codes.bitcast(FP8X4), rhs_scale=scales, start=True, stop=True,
             )
 
         def finish(name, acc, cols):
-            result = tile(name, [P, 2 * P], F32)
+            result = tile(name, [P, cols.stop - cols.start], F32)
             nc.vector.tensor_tensor(result[:], acc[:], res_sb[:, cols], ALU.add)
             nc.sync.dma_start(out=out[:, cols], in_=result[:])
 
-        gq_low = ps.tile([P, 2 * P], F32, name="gq_low", tag="a")
-        product(gq_low[:], kt01_codes[:], kt01_scales[:])
-        gq_high = ps.tile([P, 2 * P], F32, name="gq_high", tag="c0")
-        product(gq_high[:, 0:P], gk_codes[:, P : 2 * P], gk_scales[:, P : 2 * P])
-        product(gq_high[:, P : 2 * P], kt3_codes[:], kt3_scales[:])
-        finish("result_low", gq_low, slice(0, 2 * P))
-        finish("result_high", gq_high, slice(2 * P, 4 * P))
+        gq_first = ps.tile([P, 3 * P], F32, name="gq_first", tag="a")
+        product(gq_first[:, 0 : 2 * P], first_codes[:, P : 3 * P], first_scales[:, P : 3 * P])
+        product(gq_first[:, 2 * P : 3 * P], first_codes[:, 3 * P : 4 * P], first_scales[:, 3 * P : 4 * P])
+        gq_last = ps.tile([P, P], F32, name="gq_last", tag="c0")
+        product(gq_last[:], last_codes[:], last_scales[:])
+        finish("result_first", gq_first, slice(0, 3 * P))
+        finish("result_last", gq_last, slice(3 * P, 4 * P))

@@ -41,7 +41,8 @@ def tile_attend_bspanread_q_kernel(tc, query, keys_words, keys_scales, gout, val
         half = T // 2
         rows0_low = late.tile([P, half], F32, name="rows0_low", align_bytes=64, offset=4096)
         rows0_high = tile("rows0_high", [P, half], F32)
-        rows = [None] + [tile("rows%d" % b, [P, T], F32) for b in range(1, 4)]
+        rows = [None, tile("rows1", [P, T], F32), tile("rows2", [P, T], F32)]
+        rows.append(late.tile([P, T], F32, name="rows3", align_bytes=64, offset=8192))
         res_sb = tile("res_sb", [P, D], F32)
         size_col = tile("size_col", [P, PACK], F32)
         fs_col = tile("fs_col", [P, PACK], F32)
@@ -67,12 +68,13 @@ def tile_attend_bspanread_q_kernel(tc, query, keys_words, keys_scales, gout, val
         nc.sync.dma_start(out=g_raw[:], in_=gout.rearrange("(p j) w -> p (j w)", j=PACK))
         nc.scalar.activation(warm_out[:], warm_in[:], ACT.Exp)
         nc.gpsimd.dma_start(out=size_col[:], in_=size.rearrange("o (p t) -> (o p) t", t=PACK))
-        nc.sync.dma_start(out=rows0_low[:], in_=keyrows[0:P, 0:half])
         load_scales([nc.sync] * 4, vs_pool, vals_scales)
-        nc.sync.dma_start(out=rows0_high[:], in_=keyrows[0:P, half:T])
+        nc.sync.dma_start(out=rows0_low[:], in_=keyrows[0:P, 0:half])
         nc.gpsimd.dma_start(out=fs_col[:], in_=fs.rearrange("o (p t) -> (o p) t", t=PACK))
         for b in range(1, 4):
             nc.sync.dma_start(out=rows[b][:], in_=keyrows[b * P : (b + 1) * P, :])
+            if b == 1:
+                nc.sync.dma_start(out=rows0_high[:], in_=keyrows[0:P, half:T])
         nc.sync.dma_start(out=res_sb[:], in_=res)
         ones = tile("ones", [P, 32], F32)
         count = tile("count", [P, 32], F32)
@@ -152,7 +154,7 @@ def tile_attend_bspanread_q_kernel(tc, query, keys_words, keys_scales, gout, val
         p2 = late.tile([P, P], F32, name="p2", align_bytes=64, offset=4096)
         z2 = tile("z2", [P, 1], F32)
         nc.scalar.activation(pairs(p2), twice(s_neg), ACT.Exp, bias=m_neg[:], scale=-1.0, accum_out=z2[:])
-        rest = late.tile([P, I], F32, name="rest", align_bytes=64, offset=4096 + 512)
+        rest = tile("rest", [P, I], F32)
         nc.scalar.activation(rest[:], th[:], ACT.Identity, bias=4.0, scale=-4.0)
 
         drr = tile("drr", [P, I], F32)
@@ -203,36 +205,44 @@ def tile_attend_bspanread_q_kernel(tc, query, keys_words, keys_scales, gout, val
                 in_=turned[:].rearrange("p (h d) -> p d h", h=2),
             )
 
-        first = tile("first_grouped", [P, 4 * I], BF16, after="rows2")
-        last = tile("last_grouped", [P, I], BF16)
-        gather_rows(0, first[:, I : 2 * I])
-        gather_rows(1, first[:, 2 * I : 3 * I])
+        kt01 = tile("kt01_grouped", [P, 2 * I], BF16)
+        kt2 = tile("kt2_grouped", [P, I], BF16)
+        kt3 = tile("kt3_grouped", [P, I], BF16)
+        gather_rows(0, kt01[:, 0:I])
+        gather_rows(1, kt01[:, I : 2 * I])
+        gather_rows(2, kt2[:])
+        gather_rows(3, kt3[:])
+        gt = late.tile([P, I], BF16, name="gt_grouped", align_bytes=64, offset=8192)
         nc.vector.scalar_tensor_tensor(
-            first[:, 0:I].rearrange("p (q t) -> p q t", t=PACK), da_t[:].rearrange("p (t q) -> p q t", t=PACK), 0.125,
+            gt[:].rearrange("p (q t) -> p q t", t=PACK), da_t[:].rearrange("p (t q) -> p q t", t=PACK), 0.125,
             factor[:].rearrange("p (t q) -> p q t", t=PACK), ALU.mult, ALU.mult,
         )
-        gather_rows(2, first[:, 3 * I : 4 * I])
-        gather_rows(3, last[:])
-        first_codes = tile("first_codes", [P, I], U32, after="rows3")
-        first_scales = quantize("first_scales", first, first_codes)
-        last_codes = tile("last_codes", [P, P], U32)
-        last_scales = quantize("last_scales", last, last_codes)
+        codes = late.tile([P, 5 * P], U32, name="codes", align_bytes=64, offset=8192 + 1024)
+        scales = tile("scales", [P, 5 * P], U8)
 
-        def product(acc, codes, scales):
+        def quantize_into(cols, grouped):
+            nc.vector.quantize_mx(out=codes[:, cols].bitcast(FP8X4), scales=scales[:, cols], in_=grouped[:])
+
+        def product(acc, cols):
             nc.tensor.matmul_mx(
-                out=acc, lhsT=first_codes[:, 0:P].bitcast(FP8X4), lhsT_scale=first_scales[:, 0:P],
-                rhs=codes.bitcast(FP8X4), rhs_scale=scales, start=True, stop=True,
+                out=acc, lhsT=codes[:, 0:P].bitcast(FP8X4), lhsT_scale=scales[:, 0:P],
+                rhs=codes[:, cols].bitcast(FP8X4), rhs_scale=scales[:, cols], start=True, stop=True,
             )
+
+        quantize_into(slice(P, 3 * P), kt01)
+        quantize_into(slice(0, P), gt)
+        quantize_into(slice(3 * P, 4 * P), kt2)
+        quantize_into(slice(4 * P, 5 * P), kt3)
 
         def finish(name, acc, cols):
             result = tile(name, [P, cols.stop - cols.start], F32)
             nc.vector.tensor_tensor(result[:], acc[:], res_sb[:, cols], ALU.add)
             nc.sync.dma_start(out=out[:, cols], in_=result[:])
 
-        gq_first = ps.tile([P, 3 * P], F32, name="gq_first", tag="a")
-        product(gq_first[:, 0 : 2 * P], first_codes[:, P : 3 * P], first_scales[:, P : 3 * P])
-        product(gq_first[:, 2 * P : 3 * P], first_codes[:, 3 * P : 4 * P], first_scales[:, 3 * P : 4 * P])
-        gq_last = ps.tile([P, P], F32, name="gq_last", tag="c0")
-        product(gq_last[:], last_codes[:], last_scales[:])
-        finish("result_first", gq_first, slice(0, 3 * P))
-        finish("result_last", gq_last, slice(3 * P, 4 * P))
+        gq_low = ps.tile([P, 2 * P], F32, name="gq_low", tag="a")
+        product(gq_low[:], slice(P, 3 * P))
+        gq_high = ps.tile([P, 2 * P], F32, name="gq_high", tag="c0")
+        product(gq_high[:, 0:P], slice(3 * P, 4 * P))
+        product(gq_high[:, P : 2 * P], slice(4 * P, 5 * P))
+        finish("result_low", gq_low, slice(0, 2 * P))
+        finish("result_high", gq_high, slice(2 * P, 4 * P))

@@ -2,11 +2,13 @@ from contextlib import ExitStack
 
 import concourse.mybir as mybir
 
-D, T, I, Q, G = 512, 2048, 512, 128, 64
+D, T, SLOTS, Q, SPANS = 512, 2048, 512, 128, 64
 P = 128
-PACK = 4
-SPAN = I // G
-FLOPS = 3 * 2 * 512 * 128 * 512
+PLACES = 4
+QUAD = 32
+SPAN = SLOTS // SPANS
+BLOCKS = D // P
+FLOPS = 3 * 2 * D * Q * SLOTS
 
 F32 = mybir.dt.float32
 BF16 = mybir.dt.bfloat16
@@ -20,229 +22,224 @@ ALU = mybir.AluOpType
 ACT = mybir.ActivationFunctionType
 AX = mybir.AxisListType
 
+VAL_SCALES_AT = 0
+LAST_ROWS_AT = 4096
 
-def tile_attend_bspanread_q_kernel(tc, query, keys_words, keys_scales, gout, vals_words, vals_scales, size, fs, keyrows, res, offs, out):
+
+def tile_attend_bspanread_q_kernel(
+    tc, query, keys_words, keys_scales, gout, vals_words, vals_scales, size, fs, keyrows, res, offs, out
+):
     nc = tc.nc
     with ExitStack() as ctx:
         sb = ctx.enter_context(tc.tile_pool(name="sb", bufs=1))
-        late = ctx.enter_context(tc.tile_pool(name="late", bufs=1))
+        placed = ctx.enter_context(tc.tile_pool(name="placed", bufs=1))
         ps = ctx.enter_context(tc.psum_pool(name="ps", bufs=1))
 
-        def tile(name, shape, dtype, after=None):
-            return sb.tile(shape, dtype, name=name, tag=after or name, align_bytes=64)
+        def tile(name, shape, dtype, on=None):
+            return sb.tile(shape, dtype, name=name, tag=on or name, align_bytes=64)
 
-        offsets = sb.tile([P, I // 16], U16, name="offsets")
-        ks_pool = tile("ks_pool", [P, T], U8)
-        vs_pool = late.tile([P, T], U8, name="vs_pool", align_bytes=64, offset=0)
-        kw_pool = tile("kw_pool", [P, T], U16)
-        vw_pool = tile("vw_pool", [P, T], U16)
-        q_raw = tile("q_raw", [P, PACK * Q], F32)
-        g_raw = tile("g_raw", [P, PACK * Q], F32)
-        half = T // 2
-        rows0_low = late.tile([P, half], F32, name="rows0_low", align_bytes=64, offset=4096)
-        rows0_high = tile("rows0_high", [P, half], F32)
-        rows = [None, tile("rows1", [P, T], F32), tile("rows2", [P, T], F32)]
-        rows.append(late.tile([P, T], F32, name="rows3", align_bytes=64, offset=8192))
+        def tile_at(name, shape, dtype, offset):
+            return placed.tile(shape, dtype, name=name, align_bytes=64, offset=offset)
+
+        def from_slot_order(bank):
+            return bank[:].rearrange("q (p t) -> q t p", t=PLACES)
+
+        def by_place(x):
+            return x[:].rearrange("q (t p) -> q t p", t=PLACES)
+
+        def place_innermost(x):
+            return x[:].rearrange("p (t q) -> p q t", t=PLACES)
+
+        def twice(x):
+            return x[:].unsqueeze(2).to_broadcast([P, SPANS, 2])
+
+        def in_pairs(x):
+            return x[:].rearrange("q (g h) -> q g h", h=2)
+
+        def part(j):
+            return slice(j * P, (j + 1) * P)
+
+        offsets = sb.tile([P, SLOTS // 16], U16, name="offsets")
+        key_scale_pool = tile("key_scale_pool", [P, T], U8)
+        val_scale_pool = tile_at("val_scale_pool", [P, T], U8, VAL_SCALES_AT)
+        key_word_pool = tile("key_word_pool", [P, T], U16)
+        val_word_pool = tile("val_word_pool", [P, T], U16)
+        query_raw = tile("query_raw", [P, PLACES * Q], F32)
+        gout_raw = tile("gout_raw", [P, PLACES * Q], F32)
+        rows = [tile("rows%d" % b, [P, T], F32) for b in range(BLOCKS - 1)]
+        rows.append(tile_at("rows_last", [P, T], F32, LAST_ROWS_AT))
         res_sb = tile("res_sb", [P, D], F32)
-        size_col = tile("size_col", [P, PACK], F32)
-        fs_col = tile("fs_col", [P, PACK], F32)
+        size_col = tile("size_col", [P, PLACES], F32)
+        fs_col = tile("fs_col", [P, PLACES], F32)
         ident = tile("ident", [P, P], F32)
-        warm_in = tile("warm_in", [P, 1], F32)
-        warm_out = tile("warm_out", [P, 1], F32)
+        zero = tile("zero", [P, 1], F32)
+        one = tile("one", [P, 1], F32)
 
-        def load_scales(queues, pool_tile, scales):
+        def load_scale_rows(pool_tile, scales):
             for r in range(4):
-                queues[r].dma_start(
-                    out=pool_tile[r:P:32, :].bitcast(I32),
-                    in_=scales[0, r:16:4, :].bitcast(I32),
-                )
+                nc.sync.dma_start(out=pool_tile[r:P:QUAD, :].bitcast(I32), in_=scales[0, r:16:4, :].bitcast(I32))
 
-        nc.vector.memset(ks_pool[:].bitcast(I32), 0)
-        nc.vector.memset(warm_in[:], 0.0)
-        nc.vector.memset(vs_pool[:].bitcast(I32), 0)
+        nc.vector.memset(key_scale_pool[:].bitcast(I32), 0)
+        nc.vector.memset(zero[:], 0.0)
+        nc.vector.memset(val_scale_pool[:].bitcast(I32), 0)
         nc.sync.dma_start(offsets[:], offs)
-        nc.sync.dma_start(out=kw_pool[:].bitcast(I32), in_=keys_words[0].bitcast(I32))
-        load_scales([nc.sync] * 4, ks_pool, keys_scales)
-        nc.sync.dma_start(out=vw_pool[:].bitcast(I32), in_=vals_words[0].bitcast(I32))
-        nc.sync.dma_start(out=q_raw[:], in_=query.rearrange("(p j) w -> p (j w)", j=PACK))
-        nc.sync.dma_start(out=g_raw[:], in_=gout.rearrange("(p j) w -> p (j w)", j=PACK))
-        nc.scalar.activation(warm_out[:], warm_in[:], ACT.Exp)
-        nc.gpsimd.dma_start(out=size_col[:], in_=size.rearrange("o (p t) -> (o p) t", t=PACK))
-        load_scales([nc.sync] * 4, vs_pool, vals_scales)
-        nc.sync.dma_start(out=rows0_low[:], in_=keyrows[0:P, 0:half])
-        nc.gpsimd.dma_start(out=fs_col[:], in_=fs.rearrange("o (p t) -> (o p) t", t=PACK))
-        for b in range(1, 4):
-            nc.sync.dma_start(out=rows[b][:], in_=keyrows[b * P : (b + 1) * P, :])
-            if b == 1:
-                nc.sync.dma_start(out=rows0_high[:], in_=keyrows[0:P, half:T])
+        nc.sync.dma_start(out=key_word_pool[:].bitcast(I32), in_=keys_words[0].bitcast(I32))
+        load_scale_rows(key_scale_pool, keys_scales)
+        nc.sync.dma_start(out=val_word_pool[:].bitcast(I32), in_=vals_words[0].bitcast(I32))
+        nc.sync.dma_start(out=query_raw[:], in_=query.rearrange("(p t) q -> p (t q)", t=PLACES))
+        nc.sync.dma_start(out=gout_raw[:], in_=gout.rearrange("(p t) q -> p (t q)", t=PLACES))
+        nc.scalar.activation(one[:], zero[:], ACT.Exp)
+        nc.gpsimd.dma_start(out=size_col[:], in_=size.rearrange("o (p t) -> (o p) t", t=PLACES))
+        load_scale_rows(val_scale_pool, vals_scales)
+        nc.gpsimd.dma_start(out=fs_col[:], in_=fs.rearrange("o (p t) -> (o p) t", t=PLACES))
+        for b in (1, 0, 2, 3):
+            nc.sync.dma_start(out=rows[b][:], in_=keyrows[part(b), :])
         nc.sync.dma_start(out=res_sb[:], in_=res)
-        ones = tile("ones", [P, 32], F32)
-        count = tile("count", [P, 32], F32)
-        count_t = tile("count_t", [P, 32], F32)
+
+        ones = tile("ones", [P, QUAD], F32)
+        count = tile("count", [P, QUAD], F32)
+        count_turned = tile("count_turned", [P, QUAD], F32)
         nc.vector.memset(ones[:], 1.0)
         nc.vector.memset(ident[:], 0.0)
         nc.vector.tensor_tensor_scan(count[:], ones[:], ones[:], 0.0, ALU.mult, ALU.add)
-        nc.vector.transpose(count_t[:], count[:])
-        for quad in range(4):
-            part = slice(32 * quad, 32 * quad + 32)
-            nc.vector.tensor_tensor(ident[part, part], count[part, :], count_t[part, :], ALU.is_equal)
+        nc.vector.transpose(count_turned[:], count[:])
+        for quad in range(P // QUAD):
+            band = slice(QUAD * quad, QUAD * (quad + 1))
+            nc.vector.tensor_tensor(ident[band, band], count[band, :], count_turned[band, :], ALU.is_equal)
 
-        def quantize(name, grouped, codes):
-            scales = tile(name, [P, codes.shape[1]], U8)
+        def gather(name, window, dtype):
+            picked = tile(name, [P, SLOTS], dtype)
+            nc.vector.tensor_copy(picked[:], window[:].indirect(offsets[:]))
+            return picked
+
+        def quantize_columns(name, raw, codes):
+            grouped = tile(name + "_grouped", [P, PLACES * Q], BF16)
+            nc.scalar.copy(out=grouped[:].rearrange("p (q t) -> p q t", t=PLACES), in_=place_innermost(raw))
+            scales = tile(name + "_scales", [P, Q], U8)
             nc.vector.quantize_mx(out=codes[:].bitcast(FP8X4), scales=scales[:], in_=grouped[:])
             return scales
 
-        def group_rows(name, raw):
-            grouped = tile(name, [P, PACK * Q], BF16)
-            nc.scalar.copy(
-                out=grouped[:].rearrange("p (w j) -> p w j", j=PACK),
-                in_=raw[:].rearrange("p (j w) -> p w j", j=PACK),
-            )
-            return grouped
-
-        def gather(name, pool_tile, dtype):
-            picked = tile(name, [P, I], dtype)
-            nc.vector.tensor_copy(picked[:], pool_tile[:].indirect(offsets[:]))
-            return picked
-
-        def scores(name, codes, code_scales, words, scales):
-            acc = ps.tile([P, I], F32, name=name)
+        def against_listed(name, codes, code_scales, words, word_scales):
+            bank = ps.tile([P, SLOTS], F32, name=name)
             nc.tensor.matmul_mx(
-                out=acc[:], lhsT=codes[:].bitcast(FP8X4), lhsT_scale=code_scales[:],
-                rhs=words[:].bitcast(FP4X4), rhs_scale=scales[:], start=True, stop=True,
+                out=bank[:], lhsT=codes[:].bitcast(FP8X4), lhsT_scale=code_scales[:],
+                rhs=words[:].bitcast(FP4X4), rhs_scale=word_scales[:], start=True, stop=True,
             )
-            return acc
+            return bank
 
-        def dealt(acc):
-            return acc[:].rearrange("q (p t) -> q t p", t=PACK)
+        key_words = gather("key_words", key_word_pool, U16)
+        key_scales = gather("key_scales", key_scale_pool, U8)
+        val_words = gather("val_words", val_word_pool, U16)
+        query_codes = tile("query_codes", [P, Q], U32)
+        query_scales = quantize_columns("query", query_raw, query_codes)
+        a = against_listed("a", query_codes, query_scales, key_words, key_scales)
+        size_rows = ps.tile([P, SLOTS], F32, name="size_rows", tag="spread")
+        for t in range(PLACES):
+            nc.tensor.transpose(size_rows[:, part(t)], size_col[:, t : t + 1].to_broadcast([P, P]), ident[:])
+        val_scales = gather("val_scales", val_scale_pool, U8)
+        gout_codes = tile_at("gout_codes", [P, Q], U32, VAL_SCALES_AT)
+        gout_scales = quantize_columns("gout", gout_raw, gout_codes)
+        c0 = against_listed("c0", gout_codes, gout_scales, val_words, val_scales)
 
-        def by_place(x):
-            return x[:].rearrange("q (t p) -> q t p", t=PACK)
-
-        kw = gather("kw", kw_pool, U16)
-        ks = gather("ks", ks_pool, U8)
-        vw = gather("vw", vw_pool, U16)
-        q_codes = tile("q_codes", [P, Q], U32)
-        q_scales = quantize("q_scales", group_rows("q_grouped", q_raw), q_codes)
-        a = scores("a", q_codes, q_scales, kw, ks)
-        size_ps = ps.tile([P, I], F32, name="size_ps", tag="small")
-        for t in range(PACK):
-            nc.tensor.transpose(size_ps[:, t * P : (t + 1) * P], size_col[:, t : t + 1].to_broadcast([P, P]), ident[:])
-        vs = gather("vs", vs_pool, U8)
-        g_codes = late.tile([P, Q], U32, name="g_codes", align_bytes=64, offset=0)
-        g_scales = quantize("g_scales", group_rows("g_grouped", g_raw), g_codes)
-        c0 = scores("c0", g_codes, g_scales, vw, vs)
-
-        th = tile("th", [P, I], F32)
-        nc.scalar.activation(by_place(th), dealt(a), ACT.Tanh, scale=0.5)
-        s_sum = late.tile([P, G], F32, name="s_sum", align_bytes=64, offset=512)
-        nc.vector.tensor_reduce(s_sum[:], a[:].rearrange("q (g j) -> q g j", j=SPAN), AX.X, ALU.add)
-        u = late.tile([P, I], F32, name="u", align_bytes=64, offset=1024)
-        nc.vector.scalar_tensor_tensor(u[:], th[:], 1.0, size_ps[:], ALU.add, ALU.mult)
-        s_neg = tile("s_neg", [P, G], F32)
-        m_neg = tile("m_neg", [P, 1], F32)
-        nc.vector.tensor_scalar(s_neg[:], s_sum[:], -1.0 / SPAN, None, ALU.mult, ALU.min, accum_out=m_neg[:])
-        rows_bf = tile("rows_bf", [P, T], BF16)
-        nc.scalar.copy(out=rows_bf[:, 0:half], in_=rows0_low[:])
-
-        def twice(x):
-            return x[:].unsqueeze(2).to_broadcast([P, G, 2])
-
-        def pairs(x):
-            return x[:].rearrange("q (g h) -> q g h", h=2)
-
-        p2 = late.tile([P, P], F32, name="p2", align_bytes=64, offset=4096)
+        th = tile("th", [P, SLOTS], F32)
+        nc.scalar.activation(by_place(th), from_slot_order(a), ACT.Tanh, scale=0.5)
+        span_sum = tile_at("span_sum", [P, SPANS], F32, VAL_SCALES_AT + 512)
+        nc.vector.tensor_reduce(span_sum[:], a[:].rearrange("q (g j) -> q g j", j=SPAN), AX.X, ALU.add)
+        gate = tile_at("gate", [P, SLOTS], F32, VAL_SCALES_AT + 1024)
+        nc.vector.scalar_tensor_tensor(gate[:], th[:], one[:], size_rows[:], ALU.add, ALU.mult)
+        neg_s = tile("neg_s", [P, SPANS], F32)
+        neg_max = tile("neg_max", [P, 1], F32)
+        nc.vector.tensor_scalar(neg_s[:], span_sum[:], -1.0 / SPAN, None, ALU.mult, ALU.min, accum_out=neg_max[:])
+        rest4 = tile("rest4", [P, SLOTS], F32)
+        nc.scalar.activation(rest4[:], th[:], ACT.Identity, bias=4.0, scale=-4.0)
+        p_twice = tile("p_twice", [P, P], F32)
         z2 = tile("z2", [P, 1], F32)
-        nc.scalar.activation(pairs(p2), twice(s_neg), ACT.Exp, bias=m_neg[:], scale=-1.0, accum_out=z2[:])
-        rest = tile("rest", [P, I], F32)
-        nc.scalar.activation(rest[:], th[:], ACT.Identity, bias=4.0, scale=-4.0)
+        nc.scalar.activation(in_pairs(p_twice), twice(neg_s), ACT.Exp, bias=neg_max[:], scale=-1.0, accum_out=z2[:])
+        p_turned = ps.tile([P, P], F32, name="p_turned", tag="spread")
+        nc.tensor.transpose(p_turned[:], p_twice[:], ident[:])
 
-        drr = tile("drr", [P, I], F32)
-        nc.vector.tensor_tensor(by_place(drr), dealt(c0), by_place(u), ALU.mult)
-        rz = tile("rz", [P, 1], F32)
-        nc.vector.reciprocal(rz[:], z2[:])
-        r2 = tile("r2", [P, P], F32)
-        nc.scalar.activation(r2[:], p2[:], ACT.Copy, scale=rz[:])
-        p_t = ps.tile([P, P], F32, name="p_t", tag="small")
-        nc.tensor.transpose(p_t[:], r2[:], ident[:])
-        y = tile("y", [P, I], F32)
-        nc.gpsimd.tensor_tensor(y[:], rest[:], drr[:], ALU.mult)
-        dr = tile("dr", [P, G], F32)
-        nc.vector.tensor_reduce(dr[:], drr[:].rearrange("q (t g h) -> q g t h", t=PACK, h=2), AX.XY, ALU.add)
-        picked1 = gather("picked1", rows[1], BF16)
-        e = tile("e", [P, P], F32, after="rows1")
-        e_sum = tile("e_sum", [P, 1], F32)
-        nc.vector.scalar_tensor_tensor(pairs(e), twice(dr), rz[:], pairs(p2), ALU.mult, ALU.mult, accum_out=e_sum[:])
-        f2 = tile("f2", [P, P], F32)
-        nc.vector.tensor_scalar(pairs(f2), twice(dr), e_sum[:], None, ALU.subtract)
-        da_t = ps.tile([P, I], F32, name="da_t")
-        for t in range(PACK):
-            nc.tensor.matmul(da_t[:, t * P : (t + 1) * P], y[:, t * P : (t + 1) * P], ident[:],
-                             start=(t == 0), stop=False, is_transpose=True)
-        for t in range(PACK):
-            nc.tensor.matmul(da_t[:, t * P : (t + 1) * P], f2[:], ident[:],
-                             start=False, stop=(t == PACK - 1), is_transpose=True)
+        drr2 = tile("drr2", [P, SLOTS], F32)
+        nc.vector.tensor_tensor(by_place(drr2), from_slot_order(c0), by_place(gate), ALU.mult)
+        inv_z2 = tile("inv_z2", [P, 1], F32)
+        nc.vector.reciprocal(inv_z2[:], z2[:])
+        dr2 = tile("dr2", [P, SPANS], F32)
+        nc.vector.tensor_reduce(dr2[:], drr2[:].rearrange("q (t g h) -> q g t h", t=PLACES, h=2), AX.XY, ALU.add)
+        slot_term = tile("slot_term", [P, SLOTS], F32)
+        nc.vector.scalar_tensor_tensor(slot_term[:], rest4[:], inv_z2[:], drr2[:], ALU.mult, ALU.mult)
+        weighted = tile("weighted", [P, P], F32)
+        mean2 = tile("mean2", [P, 1], F32)
+        nc.vector.scalar_tensor_tensor(
+            in_pairs(weighted), twice(dr2), inv_z2[:], in_pairs(p_twice), ALU.mult, ALU.mult, accum_out=mean2[:]
+        )
+        picked_rows = {1: gather("picked1", rows[1], BF16)}
+        span_term = tile("span_term", [P, P], F32)
+        nc.vector.tensor_scalar(in_pairs(span_term), twice(dr2), mean2[:], inv_z2[:], ALU.subtract, ALU.mult)
 
-        nc.scalar.copy(out=rows_bf[:, half:T], in_=rows0_high[:])
-        factor = tile("factor", [P, I], F32, after="rows0_high")
-        for t in range(PACK):
-            nc.scalar.activation(factor[:, t * P : (t + 1) * P], p_t[:], ACT.Copy, scale=fs_col[:, t : t + 1])
+        bracket = ps.tile([P, SLOTS], F32, name="bracket")
+        for t in range(PLACES):
+            nc.tensor.matmul(
+                bracket[:, part(t)], slot_term[:, part(t)], ident[:], start=(t == 0), stop=False, is_transpose=True
+            )
+        for t in range(PLACES):
+            nc.tensor.matmul(
+                bracket[:, part(t)], span_term[:], ident[:], start=False, stop=(t == PLACES - 1), is_transpose=True
+            )
 
-        def gather_rows(b, grouped):
-            if b == 0:
-                picked = tile("picked%d" % b, [P, I], BF16)
-                nc.scalar.activation(picked[:], rows_bf[:].indirect(offsets[:]), ACT.Copy)
-            elif b == 1:
-                picked = picked1
-            else:
-                picked = gather("picked%d" % b, rows[b], BF16)
-            turned = ps.tile([P, 2 * P], F32, name="turned", tag="turned", bufs=4)
+        rows0_bf16 = tile("rows0_bf16", [P, T], BF16)
+        nc.scalar.copy(out=rows0_bf16[:], in_=rows[0][:])
+        p_fs = tile("p_fs", [P, SLOTS], F32, on="rows0")
+        for t in range(PLACES):
+            nc.scalar.activation(p_fs[:, part(t)], p_turned[:], ACT.Copy, scale=fs_col[:, t : t + 1])
+        picked_rows[0] = tile("picked0", [P, SLOTS], BF16)
+        nc.scalar.activation(picked_rows[0][:], rows0_bf16[:].indirect(offsets[:]), ACT.Copy)
+
+        def turn_rows(picked, grouped):
+            turned = ps.tile([P, 2 * P], F32, name="turned", tag="turned", bufs=BLOCKS)
             words = picked[:].bitcast(F32)
             for h in range(2):
-                nc.tensor.transpose(turned[:, h * P : (h + 1) * P], words[:, h : 2 * P : 2], ident[:])
+                nc.tensor.transpose(turned[:, part(h)], words[:, h : 2 * P : 2], ident[:])
             nc.scalar.copy(
                 out=grouped.bitcast(F32).rearrange("p (d h) -> p d h", h=2),
                 in_=turned[:].rearrange("p (h d) -> p d h", h=2),
             )
 
-        kt01 = tile("kt01_grouped", [P, 2 * I], BF16)
-        kt2 = tile("kt2_grouped", [P, I], BF16)
-        kt3 = tile("kt3_grouped", [P, I], BF16)
-        gather_rows(0, kt01[:, 0:I])
-        gather_rows(1, kt01[:, I : 2 * I])
-        gather_rows(2, kt2[:])
-        gather_rows(3, kt3[:])
-        gt = late.tile([P, I], BF16, name="gt_grouped", align_bytes=64, offset=8192)
-        nc.vector.scalar_tensor_tensor(
-            gt[:].rearrange("p (q t) -> p q t", t=PACK), da_t[:].rearrange("p (t q) -> p q t", t=PACK), 0.125,
-            factor[:].rearrange("p (t q) -> p q t", t=PACK), ALU.mult, ALU.mult,
-        )
-        codes = late.tile([P, 5 * P], U32, name="codes", align_bytes=64, offset=8192 + 1024)
-        scales = tile("scales", [P, 5 * P], U8)
+        kt01 = tile("kt01_grouped", [P, 2 * SLOTS], BF16)
+        kt2 = tile("kt2_grouped", [P, SLOTS], BF16)
+        kt3 = tile("kt3_grouped", [P, SLOTS], BF16)
+        turn_rows(picked_rows[0], kt01[:, 0:SLOTS])
+        turn_rows(picked_rows[1], kt01[:, SLOTS : 2 * SLOTS])
+        turn_rows(gather("picked2", rows[2], BF16), kt2[:])
+        turn_rows(gather("picked3", rows[3], BF16), kt3[:])
 
-        def quantize_into(cols, grouped):
+        gt1 = tile_at("gt1_grouped", [P, SLOTS], BF16, LAST_ROWS_AT)
+        nc.vector.scalar_tensor_tensor(
+            gt1[:].rearrange("p (q t) -> p q t", t=PLACES), place_innermost(bracket), 0.125, place_innermost(p_fs),
+            ALU.mult, ALU.mult,
+        )
+        codes = tile_at("codes", [P, Q + D], U32, LAST_ROWS_AT + 1024)
+        scales = tile("scales", [P, Q + D], U8)
+
+        def features(first, last):
+            return slice(Q + first * P, Q + (last + 1) * P)
+
+        for cols, grouped in ((features(0, 1), kt01), (slice(0, Q), gt1), (features(2, 2), kt2), (features(3, 3), kt3)):
             nc.vector.quantize_mx(out=codes[:, cols].bitcast(FP8X4), scales=scales[:, cols], in_=grouped[:])
 
-        def product(acc, cols):
+        def last_product(acc, cols):
             nc.tensor.matmul_mx(
-                out=acc, lhsT=codes[:, 0:P].bitcast(FP8X4), lhsT_scale=scales[:, 0:P],
+                out=acc, lhsT=codes[:, 0:Q].bitcast(FP8X4), lhsT_scale=scales[:, 0:Q],
                 rhs=codes[:, cols].bitcast(FP8X4), rhs_scale=scales[:, cols], start=True, stop=True,
             )
 
-        quantize_into(slice(P, 3 * P), kt01)
-        quantize_into(slice(0, P), gt)
-        quantize_into(slice(3 * P, 4 * P), kt2)
-        quantize_into(slice(4 * P, 5 * P), kt3)
-
-        def finish(name, acc, cols):
-            result = tile(name, [P, cols.stop - cols.start], F32)
-            nc.vector.tensor_tensor(result[:], acc[:], res_sb[:, cols], ALU.add)
+        def add_res_and_store(name, bank, cols):
+            result = tile(name, [P, 2 * P], F32)
+            nc.vector.tensor_tensor(result[:], bank[:], res_sb[:, cols], ALU.add)
             nc.sync.dma_start(out=out[:, cols], in_=result[:])
 
         gq_low = ps.tile([P, 2 * P], F32, name="gq_low", tag="a")
-        product(gq_low[:], slice(P, 3 * P))
+        last_product(gq_low[:], features(0, 1))
         gq_high = ps.tile([P, 2 * P], F32, name="gq_high", tag="c0")
-        product(gq_high[:, 0:P], slice(3 * P, 4 * P))
-        product(gq_high[:, P : 2 * P], slice(4 * P, 5 * P))
-        finish("result_low", gq_low, slice(0, 2 * P))
-        finish("result_high", gq_high, slice(2 * P, 4 * P))
+        last_product(gq_high[:, part(0)], features(2, 2))
+        last_product(gq_high[:, part(1)], features(3, 3))
+        add_res_and_store("result_low", gq_low, slice(0, 2 * P))
+        add_res_and_store("result_high", gq_high, slice(2 * P, 4 * P))

from contextlib import ExitStack

import concourse.mybir as mybir

D, T, SLOTS, Q, SPANS = 512, 2048, 512, 128, 64
P = 128
PLACES = 4
QUAD = 32
SPAN = SLOTS // SPANS
BLOCKS = D // P
FLOPS = 3 * 2 * D * Q * SLOTS

F32 = mybir.dt.float32
BF16 = mybir.dt.bfloat16
I32 = mybir.dt.int32
U32 = mybir.dt.uint32
U16 = mybir.dt.uint16
U8 = mybir.dt.uint8
FP8X4 = mybir.dt.float8_e4m3fn_x4
FP4X4 = mybir.dt.float4_e2m1fn_x4
ALU = mybir.AluOpType
ACT = mybir.ActivationFunctionType
AX = mybir.AxisListType

VAL_SCALES_AT = 0
LAST_ROWS_AT = 4096


def tile_attend_bspanread_q_kernel(
    tc, query, keys_words, keys_scales, gout, vals_words, vals_scales, size, fs, keyrows, res, offs, out
):
    nc = tc.nc
    with ExitStack() as ctx:
        sb = ctx.enter_context(tc.tile_pool(name="sb", bufs=1))
        placed = ctx.enter_context(tc.tile_pool(name="placed", bufs=1))
        ps = ctx.enter_context(tc.psum_pool(name="ps", bufs=1))

        def tile(name, shape, dtype, on=None):
            return sb.tile(shape, dtype, name=name, tag=on or name, align_bytes=64)

        def tile_at(name, shape, dtype, offset):
            return placed.tile(shape, dtype, name=name, align_bytes=64, offset=offset)

        def from_slot_order(bank):
            return bank[:].rearrange("q (p t) -> q t p", t=PLACES)

        def by_place(x):
            return x[:].rearrange("q (t p) -> q t p", t=PLACES)

        def place_innermost(x):
            return x[:].rearrange("p (t q) -> p q t", t=PLACES)

        def twice(x):
            return x[:].unsqueeze(2).to_broadcast([P, SPANS, 2])

        def in_pairs(x):
            return x[:].rearrange("q (g h) -> q g h", h=2)

        def part(j):
            return slice(j * P, (j + 1) * P)

        offsets = sb.tile([P, SLOTS // 16], U16, name="offsets")
        key_scale_pool = tile("key_scale_pool", [P, T], U8)
        val_scale_pool = tile_at("val_scale_pool", [P, T], U8, VAL_SCALES_AT)
        key_word_pool = tile("key_word_pool", [P, T], U16)
        val_word_pool = tile("val_word_pool", [P, T], U16)
        query_raw = tile("query_raw", [P, PLACES * Q], F32)
        gout_raw = tile("gout_raw", [P, PLACES * Q], F32)
        rows = [tile("rows%d" % b, [P, T], F32) for b in range(BLOCKS - 1)]
        rows.append(tile_at("rows_last", [P, T], F32, LAST_ROWS_AT))
        res_sb = tile("res_sb", [P, D], F32)
        size_col = tile("size_col", [P, PLACES], F32)
        fs_col = tile("fs_col", [P, PLACES], F32)
        ident = tile("ident", [P, P], F32)
        zero = tile("zero", [P, 1], F32)
        one = tile("one", [P, 1], F32)

        def load_scale_rows(pool_tile, scales):
            for r in range(4):
                nc.sync.dma_start(out=pool_tile[r:P:QUAD, :].bitcast(I32), in_=scales[0, r:16:4, :].bitcast(I32))

        nc.vector.memset(key_scale_pool[:].bitcast(I32), 0)
        nc.vector.memset(zero[:], 0.0)
        nc.vector.memset(val_scale_pool[:].bitcast(I32), 0)
        nc.sync.dma_start(offsets[:], offs)
        nc.sync.dma_start(out=key_word_pool[:].bitcast(I32), in_=keys_words[0].bitcast(I32))
        load_scale_rows(key_scale_pool, keys_scales)
        nc.sync.dma_start(out=val_word_pool[:].bitcast(I32), in_=vals_words[0].bitcast(I32))
        nc.sync.dma_start(out=query_raw[:], in_=query.rearrange("(p t) q -> p (t q)", t=PLACES))
        nc.sync.dma_start(out=gout_raw[:], in_=gout.rearrange("(p t) q -> p (t q)", t=PLACES))
        nc.scalar.activation(one[:], zero[:], ACT.Exp)
        nc.gpsimd.dma_start(out=size_col[:], in_=size.rearrange("o (p t) -> (o p) t", t=PLACES))
        load_scale_rows(val_scale_pool, vals_scales)
        nc.gpsimd.dma_start(out=fs_col[:], in_=fs.rearrange("o (p t) -> (o p) t", t=PLACES))
        for b in (1, 0, 2, 3):
            nc.sync.dma_start(out=rows[b][:], in_=keyrows[part(b), :])
        nc.sync.dma_start(out=res_sb[:], in_=res)

        ones = tile("ones", [P, QUAD], F32)
        count = tile("count", [P, QUAD], F32)
        count_turned = tile("count_turned", [P, QUAD], F32)
        nc.vector.memset(ones[:], 1.0)
        nc.vector.memset(ident[:], 0.0)
        nc.vector.tensor_tensor_scan(count[:], ones[:], ones[:], 0.0, ALU.mult, ALU.add)
        nc.vector.transpose(count_turned[:], count[:])
        for quad in range(P // QUAD):
            band = slice(QUAD * quad, QUAD * (quad + 1))
            nc.vector.tensor_tensor(ident[band, band], count[band, :], count_turned[band, :], ALU.is_equal)

        def gather(name, window, dtype):
            picked = tile(name, [P, SLOTS], dtype)
            nc.vector.tensor_copy(picked[:], window[:].indirect(offsets[:]))
            return picked

        def quantize_columns(name, raw, codes):
            grouped = tile(name + "_grouped", [P, PLACES * Q], BF16)
            nc.scalar.copy(out=grouped[:].rearrange("p (q t) -> p q t", t=PLACES), in_=place_innermost(raw))
            scales = tile(name + "_scales", [P, Q], U8)
            nc.vector.quantize_mx(out=codes[:].bitcast(FP8X4), scales=scales[:], in_=grouped[:])
            return scales

        def against_listed(name, codes, code_scales, words, word_scales):
            bank = ps.tile([P, SLOTS], F32, name=name)
            nc.tensor.matmul_mx(
                out=bank[:], lhsT=codes[:].bitcast(FP8X4), lhsT_scale=code_scales[:],
                rhs=words[:].bitcast(FP4X4), rhs_scale=word_scales[:], start=True, stop=True,
            )
            return bank

        key_words = gather("key_words", key_word_pool, U16)
        key_scales = gather("key_scales", key_scale_pool, U8)
        val_words = gather("val_words", val_word_pool, U16)
        query_codes = tile("query_codes", [P, Q], U32)
        query_scales = quantize_columns("query", query_raw, query_codes)
        a = against_listed("a", query_codes, query_scales, key_words, key_scales)
        size_rows = ps.tile([P, SLOTS], F32, name="size_rows", tag="spread")
        for t in range(PLACES):
            nc.tensor.transpose(size_rows[:, part(t)], size_col[:, t : t + 1].to_broadcast([P, P]), ident[:])
        val_scales = gather("val_scales", val_scale_pool, U8)
        gout_codes = tile_at("gout_codes", [P, Q], U32, VAL_SCALES_AT)
        gout_scales = quantize_columns("gout", gout_raw, gout_codes)
        c0 = against_listed("c0", gout_codes, gout_scales, val_words, val_scales)

        th = tile("th", [P, SLOTS], F32)
        nc.scalar.activation(by_place(th), from_slot_order(a), ACT.Tanh, scale=0.5)
        span_sum = tile_at("span_sum", [P, SPANS], F32, VAL_SCALES_AT + 512)
        nc.vector.tensor_reduce(span_sum[:], a[:].rearrange("q (g j) -> q g j", j=SPAN), AX.X, ALU.add)
        gate = tile_at("gate", [P, SLOTS], F32, VAL_SCALES_AT + 1024)
        nc.vector.scalar_tensor_tensor(gate[:], th[:], one[:], size_rows[:], ALU.add, ALU.mult)
        neg_s = tile("neg_s", [P, SPANS], F32)
        neg_max = tile("neg_max", [P, 1], F32)
        nc.vector.tensor_scalar(neg_s[:], span_sum[:], -1.0 / SPAN, None, ALU.mult, ALU.min, accum_out=neg_max[:])
        rest4 = tile("rest4", [P, SLOTS], F32)
        nc.scalar.activation(rest4[:], th[:], ACT.Identity, bias=4.0, scale=-4.0)
        p_twice = tile("p_twice", [P, P], F32)
        z2 = tile("z2", [P, 1], F32)
        nc.scalar.activation(in_pairs(p_twice), twice(neg_s), ACT.Exp, bias=neg_max[:], scale=-1.0, accum_out=z2[:])
        p_turned = ps.tile([P, P], F32, name="p_turned", tag="spread")
        nc.tensor.transpose(p_turned[:], p_twice[:], ident[:])

        drr2 = tile("drr2", [P, SLOTS], F32)
        nc.vector.tensor_tensor(by_place(drr2), from_slot_order(c0), by_place(gate), ALU.mult)
        inv_z2 = tile("inv_z2", [P, 1], F32)
        nc.vector.reciprocal(inv_z2[:], z2[:])
        dr2 = tile("dr2", [P, SPANS], F32)
        nc.vector.tensor_reduce(dr2[:], drr2[:].rearrange("q (t g h) -> q g t h", t=PLACES, h=2), AX.XY, ALU.add)
        slot_term = tile("slot_term", [P, SLOTS], F32)
        nc.vector.scalar_tensor_tensor(slot_term[:], rest4[:], inv_z2[:], drr2[:], ALU.mult, ALU.mult)
        weighted = tile("weighted", [P, P], F32)
        mean2 = tile("mean2", [P, 1], F32)
        nc.vector.scalar_tensor_tensor(
            in_pairs(weighted), twice(dr2), inv_z2[:], in_pairs(p_twice), ALU.mult, ALU.mult, accum_out=mean2[:]
        )
        picked_rows = {1: gather("picked1", rows[1], BF16)}
        span_term = tile("span_term", [P, P], F32)
        nc.vector.tensor_scalar(in_pairs(span_term), twice(dr2), mean2[:], inv_z2[:], ALU.subtract, ALU.mult)

        bracket = ps.tile([P, SLOTS], F32, name="bracket")
        for t in range(PLACES):
            nc.tensor.matmul(
                bracket[:, part(t)], slot_term[:, part(t)], ident[:], start=(t == 0), stop=False, is_transpose=True
            )
        for t in range(PLACES):
            nc.tensor.matmul(
                bracket[:, part(t)], span_term[:], ident[:], start=False, stop=(t == PLACES - 1), is_transpose=True
            )

        rows0_bf16 = tile("rows0_bf16", [P, T], BF16)
        nc.scalar.copy(out=rows0_bf16[:], in_=rows[0][:])
        p_fs = tile("p_fs", [P, SLOTS], F32, on="rows0")
        for t in range(PLACES):
            nc.scalar.activation(p_fs[:, part(t)], p_turned[:], ACT.Copy, scale=fs_col[:, t : t + 1])
        picked_rows[0] = tile("picked0", [P, SLOTS], BF16)
        nc.scalar.activation(picked_rows[0][:], rows0_bf16[:].indirect(offsets[:]), ACT.Copy)

        def turn_rows(picked, grouped):
            turned = ps.tile([P, 2 * P], F32, name="turned", tag="turned", bufs=BLOCKS)
            words = picked[:].bitcast(F32)
            for h in range(2):
                nc.tensor.transpose(turned[:, part(h)], words[:, h : 2 * P : 2], ident[:])
            nc.scalar.copy(
                out=grouped.bitcast(F32).rearrange("p (d h) -> p d h", h=2),
                in_=turned[:].rearrange("p (h d) -> p d h", h=2),
            )

        kt01 = tile("kt01_grouped", [P, 2 * SLOTS], BF16)
        kt2 = tile("kt2_grouped", [P, SLOTS], BF16)
        kt3 = tile("kt3_grouped", [P, SLOTS], BF16)
        turn_rows(picked_rows[0], kt01[:, 0:SLOTS])
        turn_rows(picked_rows[1], kt01[:, SLOTS : 2 * SLOTS])
        turn_rows(gather("picked2", rows[2], BF16), kt2[:])
        turn_rows(gather("picked3", rows[3], BF16), kt3[:])

        gt1 = tile_at("gt1_grouped", [P, SLOTS], BF16, LAST_ROWS_AT)
        nc.vector.scalar_tensor_tensor(
            gt1[:].rearrange("p (q t) -> p q t", t=PLACES), place_innermost(bracket), 0.125, place_innermost(p_fs),
            ALU.mult, ALU.mult,
        )
        codes = tile_at("codes", [P, Q + D], U32, LAST_ROWS_AT + 1024)
        scales = tile("scales", [P, Q + D], U8)

        def features(first, last):
            return slice(Q + first * P, Q + (last + 1) * P)

        for cols, grouped in ((features(0, 1), kt01), (slice(0, Q), gt1), (features(2, 2), kt2), (features(3, 3), kt3)):
            nc.vector.quantize_mx(out=codes[:, cols].bitcast(FP8X4), scales=scales[:, cols], in_=grouped[:])

        def last_product(acc, cols):
            nc.tensor.matmul_mx(
                out=acc, lhsT=codes[:, 0:Q].bitcast(FP8X4), lhsT_scale=scales[:, 0:Q],
                rhs=codes[:, cols].bitcast(FP8X4), rhs_scale=scales[:, cols], start=True, stop=True,
            )

        def add_res_and_store(name, bank, cols):
            result = tile(name, [P, 2 * P], F32)
            nc.vector.tensor_tensor(result[:], bank[:], res_sb[:, cols], ALU.add)
            nc.sync.dma_start(out=out[:, cols], in_=result[:])

        gq_low = ps.tile([P, 2 * P], F32, name="gq_low", tag="a")
        last_product(gq_low[:], features(0, 1))
        gq_high = ps.tile([P, 2 * P], F32, name="gq_high", tag="c0")
        last_product(gq_high[:, part(0)], features(2, 2))
        last_product(gq_high[:, part(1)], features(3, 3))
        add_res_and_store("result_low", gq_low, slice(0, 2 * P))
        add_res_and_store("result_high", gq_high, slice(2 * P, 4 * P))
